import numpy as np
import ml_dtypes


def mxq(x, axis, fmt="e4m3"):
    dtype, down = {"e4m3": (ml_dtypes.float8_e4m3fn, 7), "e5m2": (ml_dtypes.float8_e5m2, 14)}[fmt]
    v = np.moveaxis(np.asarray(x, np.float32).astype(ml_dtypes.bfloat16).astype(np.float64), axis, -1)
    blocks = v.reshape(v.shape[:-1] + (-1, 32))
    amax = np.abs(blocks).max(-1, keepdims=True)
    byte = np.maximum(np.where(amax > 0, np.frexp(amax)[1] - 1 + 127, 0) - down, 1)
    scale = np.exp2(byte - 127.0)
    codes = (blocks / scale).astype(np.float32).astype(dtype).astype(np.float64)
    return np.moveaxis((codes * scale).reshape(v.shape), -1, axis)


WIDE = False


def mx_kscale(k):
    if not WIDE:
        return np.ones(k)
    levels = np.array([10, -10, 5, -5, 0])
    if k % 512:
        return np.exp2(np.random.permutation(np.resize(levels, k // 32))).repeat(32)
    a = np.empty((k // 512, 16))
    for p in range(k // 512):
        a[p, :8] = np.random.permutation(np.resize(levels, 8))
        for g in range(8):
            far = levels[np.abs(levels - a[p, g]) >= 10]
            a[p, g + 8] = far[np.random.randint(len(far))]
    return np.exp2(a.ravel()).repeat(32)


def f64(x):
    return np.asarray(x).astype(np.float64)


def striped(idx):
    return np.tile(idx.reshape(-1, 16).T, (8, 1)).astype(np.uint16)


def unstriped(offs):
    return offs[:16].T.reshape(-1).astype(np.int64)


E2M1 = np.array([0.0, 0.5, 1.0, 1.5, 2.0, 3.0, 4.0, 6.0, -0.0, -0.5, -1.0, -1.5, -2.0, -3.0, -4.0, -6.0])


def pack_weight(w, fmt):
    k, n = w.shape
    w = f64(np.asarray(w, np.float32).astype(ml_dtypes.bfloat16)).reshape(k // 32, 32, n)
    amax = np.abs(w).max(1)
    if fmt == "e4m3":
        byte = np.frexp(amax)[1] - 1 + 127 - 7
    else:
        mant, ex = np.frexp(amax / 6.0)
        byte = np.where(mant > 0.5, ex, ex - 1) + 127
    byte = np.clip(np.where(amax > 0, byte, 1), 1, 254)
    scaled = (w * np.exp2(127.0 - byte)[:, None, :]).reshape(k, n).astype(np.float32)
    by_word = np.ascontiguousarray(scaled.reshape(k // 512, 128, 4, n).transpose(0, 1, 3, 2))
    if fmt == "e4m3":
        words = by_word.astype(ml_dtypes.float8_e4m3fn).view(np.uint8)
    else:
        c = by_word.astype(ml_dtypes.float4_e2m1fn).view(np.uint8) & 0xF
        words = (c[..., 0::2] | (c[..., 1::2] << 4)).reshape(k // 512, 128, 2 * n)
    return np.ascontiguousarray(words), np.ascontiguousarray(byte.astype(np.uint8).reshape(k // 512, 16, n))


def unpack_weight(words, scales, fmt):
    g, _, n = scales.shape
    words = np.ascontiguousarray(words).reshape(g, 128, n, -1)
    if fmt == "e4m3":
        vals = words.view(ml_dtypes.float8_e4m3fn).astype(np.float64)
    else:
        nib = np.empty((g, 128, n, 4), np.uint8)
        nib[..., 0::2] = words & 0xF
        nib[..., 1::2] = words >> 4
        vals = E2M1[nib]
    vals = vals * np.repeat(np.exp2(scales.astype(np.float64) - 127.0), 8, axis=1)[..., None]
    return vals.transpose(0, 1, 3, 2).reshape(g * 512, n)


def gelu(v):
    return 0.5 * v * (1.0 + np.tanh(np.sqrt(2.0 / np.pi) * (v + 0.044715 * v**3)))


def twice(P):
    return np.random.permutation(np.repeat(np.arange(P), 2))


def bf(x):
    return np.asarray(x, np.float32).astype(ml_dtypes.bfloat16)


def planes(Y):
    n, m = Y.shape
    b = f64(bf(Y)).reshape(n // 32, 32, m)
    amax = np.abs(b).max(1)
    byte = np.clip(np.where(amax > 0, np.frexp(amax)[1] - 1 + 127 - 7, 1), 1, 254)
    codes = (b * np.exp2(127.0 - byte)[:, None, :]).reshape(n, m).astype(np.float32).astype(ml_dtypes.float8_e4m3fn).view(np.uint8)
    words = codes.reshape(n // 512, 128, 4, m).transpose(0, 1, 3, 2)
    return np.ascontiguousarray(words), np.ascontiguousarray(byte.astype(np.uint8).reshape(n // 512, 16, m))


K, T, S, H, P = 1024, 4096, 1024, 1024, 512

def setup_inputs():
    n = np.random.standard_normal
    s = mx_kscale(K)[:, None]
    u = mx_kscale(H)[:, None]
    d = {}
    d["tab_words"], d["tab_scales"] = pack_weight(n((K, T)) * s, "e4m3")
    d["offs"] = striped(np.random.permutation(T)[:S])
    d["pos1"] = striped(np.random.permutation(S)[:P])
    d["pos2"] = striped(np.random.permutation(S)[:P])
    d["pos3"] = striped(twice(P))
    d["w1"] = (1.4 * n((K, H)) / s / K**0.5).astype(np.float32)
    d["gain"] = (np.exp(0.3 * n(H)) * u[:, 0]).astype(np.float32)
    w2 = 1.4 * n((H, H)) * np.exp(0.8 * n(H)) / u**2 / H**0.5
    d["w2_words"], d["w2_scales"] = pack_weight(w2, "e2m1")
    d["sv"] = (0.8 * np.exp(0.5 * n(H)) / u[:, 0]).astype(np.float32)
    return d

def reference(tab_words, tab_scales, offs, pos1, pos2, pos3, w1, gain, w2_words, w2_scales, sv):
    v = unpack_weight(tab_words, tab_scales, "e4m3")[:, unstriped(offs)]
    h = f64(gain)[:, None] * np.tanh(mxq(f64(w1), 0, "e4m3").T @ v)
    z = h[:, unstriped(pos1)] * h[:, unstriped(pos2)]
    w2 = unpack_weight(w2_words, w2_scales, "e2m1")
    con = w2.T @ mxq(z, 0, "e4m3")
    up = con[:, unstriped(pos3)]
    own = f64(sv)[:, None] * h
    y = up * own + up + own
    words, scales = planes(y)
    return y, words, scales

@@ -1,0 +1,331 @@
+from contextlib import ExitStack
+
+import concourse.mybir as mybir
+
+K, T, S, H, PAIRS = 1024, 4096, 1024, 1024, 512
+FLOPS = 2 * K * H * S + 2 * H * H * PAIRS
+
+F32 = mybir.dt.float32
+BF16 = mybir.dt.bfloat16
+I32 = mybir.dt.int32
+U32 = mybir.dt.uint32
+U16 = mybir.dt.uint16
+U8 = mybir.dt.uint8
+FP8X4 = mybir.dt.float8_e4m3fn_x4
+FP4X4 = mybir.dt.float4_e2m1fn_x4
+ACT = mybir.ActivationFunctionType
+ALU = mybir.AluOpType
+
+P = 128
+PACK = 4
+GROUP = P * PACK
+GROUPS = 2
+BANK = 512
+LIST_ROWS = 16
+PAIR_PIECE = 256
+CON_WINDOW = PAIRS + 32
+VECTOR_SHARE = 88
+OUT_PIECES = (((0, 512), (512, 1024)), ((0, 512), (512, 768), (768, 1024)))
+
+
+def entries(offsets, first, last):
+    return offsets[:, first // LIST_ROWS : last // LIST_ROWS]
+
+
+def weave(engine_copy, woven, rows):
+    engine_copy(
+        out=woven.rearrange("p (c i t) -> p c t i", i=4, t=PACK),
+        in_=rows.rearrange("p t (c i) -> p c t i", i=4),
+    )
+
+
+def tile_list_ballot_contest_codes_kernel(
+    tc, tab_words, tab_scales, offs, pos1, pos2, pos3, w1, gain, w2_words, w2_scales, sv, out_0, out_1, out_2
+):
+    nc = tc.nc
+    with ExitStack() as ctx:
+        keep = ctx.enter_context(tc.tile_pool(name="keep", bufs=1))
+        ring = ctx.enter_context(tc.tile_pool(name="ring", bufs=1))
+        psum = ctx.enter_context(tc.psum_pool(name="psum", bufs=8))
+
+        offs_sb = keep.tile([P, S // LIST_ROWS], U16, name="offs_sb")
+        pos1_sb = keep.tile([P, PAIRS // LIST_ROWS], U16, name="pos1_sb")
+        pos2_sb = keep.tile([P, PAIRS // LIST_ROWS], U16, name="pos2_sb")
+        pos3_sb = keep.tile([P, S // LIST_ROWS], U16, name="pos3_sb")
+        gain_sb = keep.tile([P, GROUPS, PACK], F32, name="gain_sb")
+        sv_sb = keep.tile([P, GROUPS, PACK], F32, name="sv_sb")
+        tab_scale_rows = ring.tile([P, T], U8, name="tab_scale_rows", tag="w1_rows1", bufs=1, align_bytes=64)
+
+        def load_table(a):
+            words = ring.tile([P, T], I32, name="tab_win", tag="wide", bufs=2)
+            nc.sync.dma_start(out=words[:], in_=tab_words[a].rearrange("p t i -> p (t i)").bitcast(I32))
+            return words
+
+        def load_w1(b, a):
+            raw = ring.tile([P, PACK, GROUP], F32, name="w1_raw", tag="w1_rows%d" % a, bufs=1, align_bytes=64)
+            block = w1[a * GROUP : (a + 1) * GROUP, b * GROUP : (b + 1) * GROUP]
+            nc.sync.dma_start(out=raw[:], in_=block.rearrange("(p j) c -> p j c", j=PACK))
+            return raw
+
+        nc.vector.memset(tab_scale_rows[32:64, :].bitcast(I32), 0)
+        nc.vector.memset(tab_scale_rows[64:, :].bitcast(I32), 0)
+        v_picked_scales = keep.tile([P, S], U8, name="v_picked_scales", align_bytes=64)
+        v_scales = keep.tile([P, S], U8, name="v_scales", align_bytes=64)
+        nc.vector.memset(v_scales[:].bitcast(I32), 0)
+
+        tab_win = {}
+        w1_raw = {}
+
+        def move_scale_rows(a, quadrant):
+            src = 16 * a + 4 * quadrant
+            dst = 32 * quadrant + 4 * a
+            nc.sync.dma_start(
+                out=v_scales[dst : dst + 4, :].bitcast(I32), in_=v_picked_scales[src : src + 4, :].bitcast(I32)
+            )
+
+        nc.sync.dma_start(
+            out=tab_scale_rows[:32, :].bitcast(I32), in_=tab_scales.rearrange("a q t -> (a q) t").bitcast(I32)
+        )
+        nc.sync.dma_start(offs_sb[:], offs)
+        tab_win[0] = load_table(0)
+        w1_raw[0, 0] = load_w1(0, 0)
+        tab_win[1] = load_table(1)
+        nc.sync.dma_start(out=gain_sb[:], in_=gain.rearrange("(b p t) -> p b t", b=GROUPS, t=PACK))
+        nc.sync.dma_start(out=sv_sb[:], in_=sv.rearrange("(b p t) -> p b t", b=GROUPS, t=PACK))
+        nc.sync.dma_start(pos1_sb[:], pos1)
+        nc.sync.dma_start(pos2_sb[:], pos2)
+        nc.sync.dma_start(pos3_sb[:], pos3)
+        nc.vector.tensor_copy(v_picked_scales[:], tab_scale_rows[:].indirect(offs_sb[:]))
+        moves = [(a, quadrant) for a in range(GROUPS) for quadrant in range(4)]
+        move_scale_rows(*moves[0])
+        w1_raw[0, 1] = load_w1(0, 1)
+        for move in moves[1:]:
+            move_scale_rows(*move)
+
+        con_win = []
+        for s in range(GROUPS * PACK):
+            win = keep.tile([P, CON_WINDOW], F32, name="con_win%d" % s)
+            nc.vector.memset(win[:, PAIRS:], 0.0)
+            con_win.append(win)
+
+        gain_sq = keep.tile([P, GROUPS, PACK], F32, name="gain_sq")
+        sv_gain = keep.tile([P, GROUPS, PACK], F32, name="sv_gain")
+        nc.vector.tensor_tensor(gain_sq[:], gain_sb[:], gain_sb[:], ALU.mult)
+        nc.vector.tensor_tensor(sv_gain[:], sv_sb[:], gain_sb[:], ALU.mult)
+        gain_sq_wide = keep.tile([P, GROUPS, PACK, PAIR_PIECE], F32, name="gain_sq_wide")
+        for b in range(GROUPS):
+            for t in range(PACK):
+                nc.vector.tensor_copy(gain_sq_wide[:, b, t, :], gain_sq[:, b, t : t + 1].to_broadcast([P, PAIR_PIECE]))
+
+        v_words = [keep.tile([P, S], I32, name="v_words%d" % a, align_bytes=64) for a in range(GROUPS)]
+
+        def gather_words(a):
+            nc.vector.tensor_copy(v_words[a][:].bitcast(U32), tab_win[a][:].bitcast(U32).indirect(offs_sb[:]))
+
+        w1_codes = {}
+        w1_scales = {}
+
+        def round_w1(b, a, vector_share, tag, bufs):
+            dealt = ring.tile([P, PACK, P, PACK], BF16, name="w1_dealt", tag=tag, bufs=bufs, align_bytes=64)
+            dst = dealt[:].rearrange("p t q j -> p q j t")
+            src = w1_raw[b, a][:].rearrange("p j (q t) -> p q j t", t=PACK)
+            if vector_share:
+                nc.vector.tensor_copy(dst[:, :vector_share], src[:, :vector_share])
+            nc.scalar.copy(dst[:, vector_share:], src[:, vector_share:])
+            return dealt
+
+        def quantise_w1(b, a, dealt):
+            codes = keep.tile([P, PACK, P], I32, name="w1_codes%d%d" % (b, a), align_bytes=64)
+            scales = keep.tile([P, PACK, P], U8, name="w1_scales%d%d" % (b, a), align_bytes=64)
+            for t in range(PACK):
+                nc.vector.quantize_mx(
+                    out=codes[:, t, :].bitcast(FP8X4),
+                    scales=scales[:, t, :],
+                    in_=dealt[:, t].rearrange("p q j -> p (q j)"),
+                )
+            w1_codes[b, a] = codes
+            w1_scales[b, a] = scales
+
+        tanh_rows = {}
+
+        def first_product(b):
+            banks = {}
+            for t in range(PACK):
+                for a in range(GROUPS):
+                    for half in range(S // BANK):
+                        if a == 0:
+                            banks[t, half] = psum.tile([P, BANK], F32, name="bank", tag="bank")
+                        cols = slice(half * BANK, (half + 1) * BANK)
+                        nc.tensor.matmul_mx(
+                            out=banks[t, half][:],
+                            lhsT=w1_codes[b, a][:, t, :].bitcast(FP8X4),
+                            lhsT_scale=w1_scales[b, a][:, t, :],
+                            rhs=v_words[a][:, cols].bitcast(FP8X4),
+                            rhs_scale=v_scales[4 * a :, cols],
+                            start=(a == 0),
+                            stop=(a == GROUPS - 1),
+                        )
+            for t in range(PACK):
+                rows = keep.tile([P, S], F32, name="tanh_rows%d%d" % (b, t))
+                for half in range(S // BANK):
+                    nc.scalar.activation(rows[:, half * BANK : (half + 1) * BANK], banks[t, half][:], ACT.Tanh)
+                tanh_rows[b, t] = rows
+
+        z_rows = {}
+
+        def pair_products(b, t):
+            if t == 0:
+                z_rows[b] = ring.tile([P, PACK, PAIRS], F32, name="z_rows", tag="rows", bufs=3)
+            firsts = []
+            for m0 in range(0, PAIRS, PAIR_PIECE):
+                first = ring.tile([P, PAIR_PIECE], F32, name="first", tag="first", bufs=4)
+                window = tanh_rows[b, t][:].indirect(entries(pos1_sb, m0, m0 + PAIR_PIECE))
+                nc.vector.tensor_tensor(first[:], window, gain_sq_wide[:, b, t, :], ALU.mult)
+                firsts.append(first)
+            for m0, first in zip(range(0, PAIRS, PAIR_PIECE), firsts):
+                window = tanh_rows[b, t][:].indirect(entries(pos2_sb, m0, m0 + PAIR_PIECE))
+                nc.vector.tensor_tensor(z_rows[b][:, t, m0 : m0 + PAIR_PIECE], window, first[:], ALU.mult)
+
+        z_codes = [keep.tile([P, PAIRS], I32, name="z_codes%d" % b, align_bytes=64) for b in range(GROUPS)]
+        z_scales = [keep.tile([P, PAIRS], U8, name="z_scales%d" % b, align_bytes=64) for b in range(GROUPS)]
+
+        def quantise_z(b, copies, tag, bufs):
+            woven = ring.tile([P, PAIRS * PACK], BF16, name="z_woven", tag=tag, bufs=bufs, align_bytes=64)
+            for m0, engine_copy in zip(range(0, PAIRS, PAIR_PIECE), copies):
+                weave(engine_copy, woven[:, m0 * PACK : (m0 + PAIR_PIECE) * PACK], z_rows[b][:, :, m0 : m0 + PAIR_PIECE])
+            for m0 in range(0, PAIRS, PAIR_PIECE):
+                nc.vector.quantize_mx(
+                    out=z_codes[b][:, m0 : m0 + PAIR_PIECE].bitcast(FP8X4),
+                    scales=z_scales[b][:, m0 : m0 + PAIR_PIECE],
+                    in_=woven[:, m0 * PACK : (m0 + PAIR_PIECE) * PACK],
+                )
+
+        w2_dealt = {}
+        w2_dealt_scales = {}
+
+        def deal_w2(b, tag):
+            both = ring.tile([P, 3 * GROUPS * GROUP], U8, name="w2_dealt", tag=tag, bufs=1, align_bytes=64)
+            words = both[:, : 2 * GROUPS * GROUP].rearrange("p (a t q e) -> p a t q e", a=GROUPS, t=PACK, e=2)
+            scales = both[:, 2 * GROUPS * GROUP :].rearrange("p (a t q) -> p a t q", a=GROUPS, t=PACK)
+            src = w2_raw[:, :, 2 * b * GROUP : 2 * (b + 1) * GROUP].rearrange("p a (q t e) -> p a t q e", t=PACK, e=2)
+            nc.vector.tensor_copy(words, src)
+            src = w2_scale_rows[:, :, b * GROUP : (b + 1) * GROUP].rearrange("p a (q t) -> p a t q", t=PACK)
+            nc.vector.tensor_copy(scales, src)
+            w2_dealt[b] = words
+            w2_dealt_scales[b] = scales
+
+        def second_product(b):
+            banks = {}
+            for a in range(GROUPS):
+                for t in range(PACK):
+                    if a == 0:
+                        banks[t] = psum.tile([P, BANK], F32, name="bank", tag="bank")
+                    nc.tensor.matmul_mx(
+                        out=banks[t][:],
+                        lhsT=w2_dealt[b][:, a, t].rearrange("p q e -> p (q e)").bitcast(FP4X4),
+                        lhsT_scale=w2_dealt_scales[b][:, a, t, :],
+                        rhs=z_codes[a][:].bitcast(FP8X4),
+                        rhs_scale=z_scales[a][:],
+                        start=(a == 0),
+                        stop=(a == GROUPS - 1),
+                    )
+            for t in range(PACK):
+                nc.scalar.copy(con_win[b * PACK + t][:, :PAIRS], banks[t][:])
+
+        one_plus_own = {}
+
+        def make_one_plus_own(b):
+            rows = ring.tile([P, PACK, S], F32, name="one_plus_own", tag="wide", bufs=2)
+            for t in range(PACK):
+                nc.scalar.activation(
+                    rows[:, t, :], tanh_rows[b, t][:], ACT.Identity, bias=1.0, scale=sv_gain[:, b, t : t + 1]
+                )
+            one_plus_own[b] = rows
+
+        gather_words(0)
+        quantise_w1(0, 0, round_w1(0, 0, 0, "hold2", 1))
+        gather_words(1)
+        quantise_w1(0, 1, round_w1(0, 1, VECTOR_SHARE, "hold3", 1))
+        w1_raw[1, 0] = load_w1(1, 0)
+        w1_raw[1, 1] = load_w1(1, 1)
+        w2_raw = ring.tile([P, GROUPS, 2 * H], U8, name="w2_raw", tag="hold2", bufs=1, align_bytes=64)
+        nc.sync.dma_start(out=w2_raw[:].bitcast(I32), in_=w2_words.rearrange("a p c -> p a c").bitcast(I32))
+        w2_scale_rows = ring.tile([P, GROUPS, H], U8, name="w2_scale_rows", tag="hold3", bufs=1, align_bytes=64)
+        nc.vector.memset(w2_scale_rows[:].rearrange("p a c -> p (a c)").bitcast(I32), 0)
+        w2_by_row = w2_scales.rearrange("a (q r) c -> r q a c", r=4)
+        for r in range(4):
+            nc.sync.dma_start(out=w2_scale_rows[r:P:32, :, :].bitcast(I32), in_=w2_by_row[r].bitcast(I32))
+        first_product(0)
+        dealt_10 = round_w1(1, 0, 0, "woven", 3)
+        dealt_11 = round_w1(1, 1, 0, "hold0", 1)
+        for t in range(PACK):
+            pair_products(0, t)
+        quantise_w1(1, 0, dealt_10)
+        quantise_w1(1, 1, dealt_11)
+        deal_w2(0, "hold0")
+        first_product(1)
+        make_one_plus_own(0)
+        for t in range(PACK):
+            pair_products(1, t)
+        quantise_z(0, (nc.scalar.copy, nc.scalar.copy), "woven", 3)
+        quantise_z(1, (nc.scalar.copy, nc.vector.tensor_copy), "hold1", 1)
+        deal_w2(1, "hold1")
+        second_product(0)
+        second_product(1)
+        make_one_plus_own(1)
+
+        y_scales = [keep.tile([P, S], U8, name="y_scales%d" % b, align_bytes=64) for b in range(GROUPS)]
+        steps = [(b, j0, j1, t) for b in range(GROUPS) for (j0, j1) in OUT_PIECES[b] for t in range(PACK)]
+        y_rows = {}
+        raised = {}
+        y_woven = {}
+
+        def raise_code(b, j0, j1, t):
+            prod = ring.tile([P, j1 - j0], F32, name="raised", tag="raised", bufs=3)
+            window = con_win[b * PACK + t][:].indirect(entries(pos3_sb, j0, j1))
+            nc.vector.tensor_tensor(prod[:], window, one_plus_own[b][:, t, j0:j1], ALU.mult)
+            raised[b, j0, t] = prod
+
+        def add_own(b, j0, j1, t):
+            if t == 0:
+                y_rows[b, j0] = ring.tile([P, PACK, j1 - j0], F32, name="y_rows", tag="rows", bufs=3)
+            nc.vector.scalar_tensor_tensor(
+                out=y_rows[b, j0][:, t, :],
+                in0=tanh_rows[b, t][:, j0:j1],
+                scalar=sv_gain[:, b, t : t + 1],
+                in1=raised[b, j0, t][:],
+                op0=ALU.mult,
+                op1=ALU.add,
+            )
+            out_rows = out_0[b * GROUP : (b + 1) * GROUP, j0:j1].rearrange("(p t) j -> t p j", t=PACK)
+            nc.sync.dma_start(out=out_rows[t], in_=y_rows[b, j0][:, t, :])
+
+        def round_y(b, j0, j1, engine_copy):
+            woven = ring.tile([P, (j1 - j0) * PACK], BF16, name="y_woven", tag="woven", bufs=3, align_bytes=64)
+            weave(engine_copy, woven[:], y_rows[b, j0][:])
+            y_woven[b, j0] = woven
+
+        def quantise_y(b, j0, j1):
+            codes = ring.tile([P, j1 - j0], I32, name="y_codes", tag="y_codes", bufs=3, align_bytes=64)
+            nc.vector.quantize_mx(out=codes[:].bitcast(FP8X4), scales=y_scales[b][:, j0:j1], in_=y_woven[b, j0][:])
+            words = out_1[b, :, j0:j1, :].rearrange("p m t -> p (m t)").bitcast(I32)
+            nc.sync.dma_start(out=words, in_=codes[:])
+            if j1 == S:
+                by_row = out_2[b].rearrange("(q r) m -> r q m", r=4)
+                for r in range(4):
+                    queue = nc.scalar if r % 2 else nc.sync
+                    queue.dma_start(out=by_row[r].bitcast(I32), in_=y_scales[b][r:P:32, :].bitcast(I32))
+
+        raise_code(*steps[0])
+        waiting = None
+        for i, (b, j0, j1, t) in enumerate(steps):
+            if i + 1 < len(steps):
+                raise_code(*steps[i + 1])
+            add_own(b, j0, j1, t)
+            if t == PACK - 1:
+                if waiting is not None:
+                    quantise_y(*waiting)
+                last = i + 1 == len(steps)
+                round_y(b, j0, j1, nc.vector.tensor_copy if last else nc.scalar.copy)
+                waiting = (b, j0, j1)
+        quantise_y(*waiting)

@@ -54,7 +54,13 @@ def tile_list_ballot_contest_codes_kernel(
         pos3_sb = keep.tile([P, S // LIST_ROWS], U16, name="pos3_sb")
         gain_sb = keep.tile([P, GROUPS, PACK], F32, name="gain_sb")
         sv_sb = keep.tile([P, GROUPS, PACK], F32, name="sv_sb")
-        tab_scale_rows = ring.tile([P, T], U8, name="tab_scale_rows", tag="w1_rows1", bufs=1, align_bytes=64)
+        tab_scale_rows = keep.tile([P, T], U8, name="tab_scale_rows", align_bytes=64)
+        w2_scale_rows = keep.tile([P, GROUPS, H], U8, name="w2_scale_rows", align_bytes=64)
+        w2_raw = [keep.tile([P, GROUPS, 2 * GROUP], U8, name="w2_raw%d" % b, align_bytes=64) for b in range(GROUPS)]
+
+        def load_w2(b):
+            block = w2_words[:, :, 2 * b * GROUP : 2 * (b + 1) * GROUP].rearrange("a p c -> p a c")
+            nc.sync.dma_start(out=w2_raw[b][:].bitcast(I32), in_=block.bitcast(I32))
 
         def load_table(a):
             words = ring.tile([P, T], I32, name="tab_win", tag="wide", bufs=2)
@@ -62,11 +68,12 @@ def tile_list_ballot_contest_codes_kernel(
             return words
 
         def load_w1(b, a):
-            raw = ring.tile([P, PACK, GROUP], F32, name="w1_raw", tag="w1_rows%d" % a, bufs=1, align_bytes=64)
+            raw = ring.tile([P, PACK, GROUP], F32, name="w1_raw", tag="rows", bufs=5)
             block = w1[a * GROUP : (a + 1) * GROUP, b * GROUP : (b + 1) * GROUP]
             nc.sync.dma_start(out=raw[:], in_=block.rearrange("(p j) c -> p j c", j=PACK))
             return raw
 
+        nc.vector.memset(w2_scale_rows[:].rearrange("p a c -> p (a c)").bitcast(I32), 0)
         nc.vector.memset(tab_scale_rows[32:64, :].bitcast(I32), 0)
         nc.vector.memset(tab_scale_rows[64:, :].bitcast(I32), 0)
         v_picked_scales = keep.tile([P, S], U8, name="v_picked_scales", align_bytes=64)
@@ -79,7 +86,7 @@ def tile_list_ballot_contest_codes_kernel(
         def move_scale_rows(a, quadrant):
             src = 16 * a + 4 * quadrant
             dst = 32 * quadrant + 4 * a
-            nc.sync.dma_start(
+            nc.gpsimd.dma_start(
                 out=v_scales[dst : dst + 4, :].bitcast(I32), in_=v_picked_scales[src : src + 4, :].bitcast(I32)
             )
 
@@ -88,19 +95,25 @@ def tile_list_ballot_contest_codes_kernel(
         )
         nc.sync.dma_start(offs_sb[:], offs)
         tab_win[0] = load_table(0)
+        load_w2(0)
         w1_raw[0, 0] = load_w1(0, 0)
         tab_win[1] = load_table(1)
+        w1_raw[0, 1] = load_w1(0, 1)
         nc.sync.dma_start(out=gain_sb[:], in_=gain.rearrange("(b p t) -> p b t", b=GROUPS, t=PACK))
         nc.sync.dma_start(out=sv_sb[:], in_=sv.rearrange("(b p t) -> p b t", b=GROUPS, t=PACK))
         nc.sync.dma_start(pos1_sb[:], pos1)
         nc.sync.dma_start(pos2_sb[:], pos2)
+        w1_raw[1, 0] = load_w1(1, 0)
+        w1_raw[1, 1] = load_w1(1, 1)
         nc.sync.dma_start(pos3_sb[:], pos3)
+        load_w2(1)
+        w2_by_row = w2_scales.rearrange("a (q r) c -> r q a c", r=4)
+        for r in range(4):
+            nc.gpsimd.dma_start(out=w2_scale_rows[r:P:32, :, :].bitcast(I32), in_=w2_by_row[r].bitcast(I32))
         nc.vector.tensor_copy(v_picked_scales[:], tab_scale_rows[:].indirect(offs_sb[:]))
-        moves = [(a, quadrant) for a in range(GROUPS) for quadrant in range(4)]
-        move_scale_rows(*moves[0])
-        w1_raw[0, 1] = load_w1(0, 1)
-        for move in moves[1:]:
-            move_scale_rows(*move)
+        for a in range(GROUPS):
+            for quadrant in range(4):
+                move_scale_rows(a, quadrant)
 
         con_win = []
         for s in range(GROUPS * PACK):
@@ -127,15 +140,15 @@ def tile_list_ballot_contest_codes_kernel(
 
         def round_w1(b, a, vector_share, tag, bufs):
             dealt = ring.tile([P, PACK, P, PACK], BF16, name="w1_dealt", tag=tag, bufs=bufs, align_bytes=64)
-            dst = dealt[:].rearrange("p t q j -> p q j t")
-            src = w1_raw[b, a][:].rearrange("p j (q t) -> p q j t", t=PACK)
+            dst = dealt[:].rearrange("p t q j -> p q t j")
+            src = w1_raw[b, a][:].rearrange("p j (q t) -> p q t j", t=PACK)
             if vector_share:
                 nc.vector.tensor_copy(dst[:, :vector_share], src[:, :vector_share])
             nc.scalar.copy(dst[:, vector_share:], src[:, vector_share:])
             return dealt
 
         def quantise_w1(b, a, dealt):
-            codes = keep.tile([P, PACK, P], I32, name="w1_codes%d%d" % (b, a), align_bytes=64)
+            codes = ring.tile([P, PACK, P], I32, name="w1_codes", tag="codes%d%d" % (b, a), bufs=1, align_bytes=64)
             scales = keep.tile([P, PACK, P], U8, name="w1_scales%d%d" % (b, a), align_bytes=64)
             for t in range(PACK):
                 nc.vector.quantize_mx(
@@ -150,8 +163,8 @@ def tile_list_ballot_contest_codes_kernel(
 
         def first_product(b):
             banks = {}
-            for t in range(PACK):
-                for a in range(GROUPS):
+            for a in range(GROUPS):
+                for t in range(PACK):
                     for half in range(S // BANK):
                         if a == 0:
                             banks[t, half] = psum.tile([P, BANK], F32, name="bank", tag="bank")
@@ -173,18 +186,18 @@ def tile_list_ballot_contest_codes_kernel(
 
         z_rows = {}
 
-        def pair_products(b, t):
+        def pair_products(b, t, tag="first", bufs=2):
             if t == 0:
-                z_rows[b] = ring.tile([P, PACK, PAIRS], F32, name="z_rows", tag="rows", bufs=3)
-            firsts = []
+                z_rows[b] = ring.tile([P, PACK, PAIRS], F32, name="z_rows", tag="rows", bufs=5)
+            first = ring.tile([P, PAIRS], F32, name="first", tag=tag, bufs=bufs, align_bytes=64)
             for m0 in range(0, PAIRS, PAIR_PIECE):
-                first = ring.tile([P, PAIR_PIECE], F32, name="first", tag="first", bufs=4)
                 window = tanh_rows[b, t][:].indirect(entries(pos1_sb, m0, m0 + PAIR_PIECE))
-                nc.vector.tensor_tensor(first[:], window, gain_sq_wide[:, b, t, :], ALU.mult)
-                firsts.append(first)
-            for m0, first in zip(range(0, PAIRS, PAIR_PIECE), firsts):
+                nc.vector.tensor_tensor(first[:, m0 : m0 + PAIR_PIECE], window, gain_sq_wide[:, b, t, :], ALU.mult)
+            for m0 in range(0, PAIRS, PAIR_PIECE):
                 window = tanh_rows[b, t][:].indirect(entries(pos2_sb, m0, m0 + PAIR_PIECE))
-                nc.vector.tensor_tensor(z_rows[b][:, t, m0 : m0 + PAIR_PIECE], window, first[:], ALU.mult)
+                nc.vector.tensor_tensor(
+                    z_rows[b][:, t, m0 : m0 + PAIR_PIECE], window, first[:, m0 : m0 + PAIR_PIECE], ALU.mult
+                )
 
         z_codes = [keep.tile([P, PAIRS], I32, name="z_codes%d" % b, align_bytes=64) for b in range(GROUPS)]
         z_scales = [keep.tile([P, PAIRS], U8, name="z_scales%d" % b, align_bytes=64) for b in range(GROUPS)]
@@ -201,18 +214,16 @@ def tile_list_ballot_contest_codes_kernel(
                 )
 
         w2_dealt = {}
-        w2_dealt_scales = {}
+        w2_dealt_scales = keep.tile([P, GROUPS * GROUPS, PACK, P], U8, name="w2_dealt_scales", align_bytes=64)
 
         def deal_w2(b, tag):
-            both = ring.tile([P, 3 * GROUPS * GROUP], U8, name="w2_dealt", tag=tag, bufs=1, align_bytes=64)
-            words = both[:, : 2 * GROUPS * GROUP].rearrange("p (a t q e) -> p a t q e", a=GROUPS, t=PACK, e=2)
-            scales = both[:, 2 * GROUPS * GROUP :].rearrange("p (a t q) -> p a t q", a=GROUPS, t=PACK)
-            src = w2_raw[:, :, 2 * b * GROUP : 2 * (b + 1) * GROUP].rearrange("p a (q t e) -> p a t q e", t=PACK, e=2)
-            nc.vector.tensor_copy(words, src)
-            src = w2_scale_rows[:, :, b * GROUP : (b + 1) * GROUP].rearrange("p a (q t) -> p a t q", t=PACK)
-            nc.vector.tensor_copy(scales, src)
+            words = ring.tile([P, GROUPS, PACK, P, 2], U8, name="w2_dealt", tag=tag, bufs=1, align_bytes=64)
+            nc.vector.tensor_copy(words[:], w2_raw[b][:].rearrange("p a (q t e) -> p a t q e", t=PACK, e=2))
             w2_dealt[b] = words
-            w2_dealt_scales[b] = scales
+
+        def deal_w2_scales():
+            src = w2_scale_rows[:].rearrange("p a (b q t) -> p (a b) t q", b=GROUPS, t=PACK)
+            nc.vector.tensor_copy(w2_dealt_scales[:], src)
 
         def second_product(b):
             banks = {}
@@ -223,7 +234,7 @@ def tile_list_ballot_contest_codes_kernel(
                     nc.tensor.matmul_mx(
                         out=banks[t][:],
                         lhsT=w2_dealt[b][:, a, t].rearrange("p q e -> p (q e)").bitcast(FP4X4),
-                        lhsT_scale=w2_dealt_scales[b][:, a, t, :],
+                        lhsT_scale=w2_dealt_scales[:, a * GROUPS + b, t, :],
                         rhs=z_codes[a][:].bitcast(FP8X4),
                         rhs_scale=z_scales[a][:],
                         start=(a == 0),
@@ -234,45 +245,40 @@ def tile_list_ballot_contest_codes_kernel(
 
         one_plus_own = {}
 
-        def make_one_plus_own(b):
-            rows = ring.tile([P, PACK, S], F32, name="one_plus_own", tag="wide", bufs=2)
-            for t in range(PACK):
+        def make_one_plus_own(b, slices):
+            if b not in one_plus_own:
+                one_plus_own[b] = ring.tile([P, PACK, S], F32, name="one_plus_own", tag="wide", bufs=2)
+            for t in slices:
                 nc.scalar.activation(
-                    rows[:, t, :], tanh_rows[b, t][:], ACT.Identity, bias=1.0, scale=sv_gain[:, b, t : t + 1]
+                    one_plus_own[b][:, t, :], tanh_rows[b, t][:], ACT.Identity, bias=1.0, scale=sv_gain[:, b, t : t + 1]
                 )
-            one_plus_own[b] = rows
 
         gather_words(0)
-        quantise_w1(0, 0, round_w1(0, 0, 0, "hold2", 1))
+        deal_w2(0, "dealt0")
+        quantise_w1(0, 0, round_w1(0, 0, 0, "woven", 3))
         gather_words(1)
-        quantise_w1(0, 1, round_w1(0, 1, VECTOR_SHARE, "hold3", 1))
-        w1_raw[1, 0] = load_w1(1, 0)
-        w1_raw[1, 1] = load_w1(1, 1)
-        w2_raw = ring.tile([P, GROUPS, 2 * H], U8, name="w2_raw", tag="hold2", bufs=1, align_bytes=64)
-        nc.sync.dma_start(out=w2_raw[:].bitcast(I32), in_=w2_words.rearrange("a p c -> p a c").bitcast(I32))
-        w2_scale_rows = ring.tile([P, GROUPS, H], U8, name="w2_scale_rows", tag="hold3", bufs=1, align_bytes=64)
-        nc.vector.memset(w2_scale_rows[:].rearrange("p a c -> p (a c)").bitcast(I32), 0)
-        w2_by_row = w2_scales.rearrange("a (q r) c -> r q a c", r=4)
-        for r in range(4):
-            nc.sync.dma_start(out=w2_scale_rows[r:P:32, :, :].bitcast(I32), in_=w2_by_row[r].bitcast(I32))
+        quantise_w1(0, 1, round_w1(0, 1, VECTOR_SHARE, "woven", 3))
+        deal_w2_scales()
         first_product(0)
-        dealt_10 = round_w1(1, 0, 0, "woven", 3)
-        dealt_11 = round_w1(1, 1, 0, "hold0", 1)
-        for t in range(PACK):
+        dealt_10 = round_w1(1, 0, 0, "codes00", 1)
+        dealt_11 = round_w1(1, 1, 48, "codes01", 1)
+        for t in range(PACK - 1):
             pair_products(0, t)
         quantise_w1(1, 0, dealt_10)
         quantise_w1(1, 1, dealt_11)
-        deal_w2(0, "hold0")
+        pair_products(0, PACK - 1, "codes01", 1)
         first_product(1)
-        make_one_plus_own(0)
-        for t in range(PACK):
+        for t in range(PACK - 1):
             pair_products(1, t)
-        quantise_z(0, (nc.scalar.copy, nc.scalar.copy), "woven", 3)
+        quantise_z(0, (nc.scalar.copy, nc.scalar.copy), "hold0", 1)
+        pair_products(1, PACK - 1, "hold0", 1)
+        make_one_plus_own(0, range(PACK - 1))
         quantise_z(1, (nc.scalar.copy, nc.vector.tensor_copy), "hold1", 1)
         deal_w2(1, "hold1")
         second_product(0)
+        make_one_plus_own(0, range(PACK - 1, PACK))
         second_product(1)
-        make_one_plus_own(1)
+        make_one_plus_own(1, range(PACK))
 
         y_scales = [keep.tile([P, S], U8, name="y_scales%d" % b, align_bytes=64) for b in range(GROUPS)]
         steps = [(b, j0, j1, t) for b in range(GROUPS) for (j0, j1) in OUT_PIECES[b] for t in range(PACK)]
@@ -288,7 +294,7 @@ def tile_list_ballot_contest_codes_kernel(
 
         def add_own(b, j0, j1, t):
             if t == 0:
-                y_rows[b, j0] = ring.tile([P, PACK, j1 - j0], F32, name="y_rows", tag="rows", bufs=3)
+                y_rows[b, j0] = ring.tile([P, PACK, j1 - j0], F32, name="y_rows", tag="rows", bufs=5)
             nc.vector.scalar_tensor_tensor(
                 out=y_rows[b, j0][:, t, :],
                 in0=tanh_rows[b, t][:, j0:j1],

@@ -34,8 +34,8 @@ def entries(offsets, first, last):
 
 def weave(engine_copy, woven, rows):
     engine_copy(
-        out=woven.rearrange("p (c i t) -> p c t i", i=4, t=PACK),
-        in_=rows.rearrange("p t (c i) -> p c t i", i=4),
+        out=woven.rearrange("p (c t) -> p c t", t=PACK),
+        in_=rows.rearrange("p t c -> p c t"),
     )
 
 
@@ -54,66 +54,58 @@ def tile_list_ballot_contest_codes_kernel(
         pos3_sb = keep.tile([P, S // LIST_ROWS], U16, name="pos3_sb")
         gain_sb = keep.tile([P, GROUPS, PACK], F32, name="gain_sb")
         sv_sb = keep.tile([P, GROUPS, PACK], F32, name="sv_sb")
-        tab_scale_rows = keep.tile([P, T], U8, name="tab_scale_rows", align_bytes=64)
-        w2_scale_rows = keep.tile([P, GROUPS, H], U8, name="w2_scale_rows", align_bytes=64)
-        w2_raw = [keep.tile([P, GROUPS, 2 * GROUP], U8, name="w2_raw%d" % b, align_bytes=64) for b in range(GROUPS)]
+        tab_scale_rows = ring.tile([P, T], U8, name="tab_scale_rows", tag="wide", bufs=2, align_bytes=64)
+        w2_raw = {}
 
-        def load_w2(b):
+        def load_w2(b, tag):
+            w2_raw[b] = ring.tile([P, GROUPS, 2 * GROUP], U8, name="w2_raw", tag=tag, bufs=1, align_bytes=64)
             block = w2_words[:, :, 2 * b * GROUP : 2 * (b + 1) * GROUP].rearrange("a p c -> p a c")
             nc.sync.dma_start(out=w2_raw[b][:].bitcast(I32), in_=block.bitcast(I32))
 
         def load_table(a):
-            words = ring.tile([P, T], I32, name="tab_win", tag="wide", bufs=2)
+            words = ring.tile([P, T], I32, name="tab_win", tag="wide", bufs=2, align_bytes=64)
             nc.sync.dma_start(out=words[:], in_=tab_words[a].rearrange("p t i -> p (t i)").bitcast(I32))
             return words
 
         def load_w1(b, a):
-            raw = ring.tile([P, PACK, GROUP], F32, name="w1_raw", tag="rows", bufs=5)
+            raw = ring.tile([P, PACK, GROUP], F32, name="w1_raw", tag="w1_rows%d" % a, bufs=1)
             block = w1[a * GROUP : (a + 1) * GROUP, b * GROUP : (b + 1) * GROUP]
             nc.sync.dma_start(out=raw[:], in_=block.rearrange("(p j) c -> p j c", j=PACK))
             return raw
 
-        nc.vector.memset(w2_scale_rows[:].rearrange("p a c -> p (a c)").bitcast(I32), 0)
         nc.vector.memset(tab_scale_rows[32:64, :].bitcast(I32), 0)
         nc.vector.memset(tab_scale_rows[64:, :].bitcast(I32), 0)
         v_picked_scales = keep.tile([P, S], U8, name="v_picked_scales", align_bytes=64)
-        v_scales = keep.tile([P, S], U8, name="v_scales", align_bytes=64)
-        nc.vector.memset(v_scales[:].bitcast(I32), 0)
+        v_scales = [keep.tile([P, S], U8, name="v_scales%d" % a, align_bytes=64) for a in range(GROUPS)]
+        for a in range(GROUPS):
+            nc.vector.memset(v_scales[a][:].bitcast(I32), 0)
 
         tab_win = {}
         w1_raw = {}
 
-        def move_scale_rows(a, quadrant):
-            src = 16 * a + 4 * quadrant
-            dst = 32 * quadrant + 4 * a
-            nc.gpsimd.dma_start(
-                out=v_scales[dst : dst + 4, :].bitcast(I32), in_=v_picked_scales[src : src + 4, :].bitcast(I32)
-            )
+        def move_scale_rows(a):
+            for quadrant in range(4):
+                src = 16 * a + 4 * quadrant
+                dst = 32 * quadrant
+                nc.sync.dma_start(
+                    out=v_scales[a][dst : dst + 4, :].bitcast(I32), in_=v_picked_scales[src : src + 4, :].bitcast(I32)
+                )
 
         nc.sync.dma_start(
             out=tab_scale_rows[:32, :].bitcast(I32), in_=tab_scales.rearrange("a q t -> (a q) t").bitcast(I32)
         )
         nc.sync.dma_start(offs_sb[:], offs)
         tab_win[0] = load_table(0)
-        load_w2(0)
+        load_w2(0, "w2_raw0")
         w1_raw[0, 0] = load_w1(0, 0)
-        tab_win[1] = load_table(1)
-        w1_raw[0, 1] = load_w1(0, 1)
         nc.sync.dma_start(out=gain_sb[:], in_=gain.rearrange("(b p t) -> p b t", b=GROUPS, t=PACK))
         nc.sync.dma_start(out=sv_sb[:], in_=sv.rearrange("(b p t) -> p b t", b=GROUPS, t=PACK))
         nc.sync.dma_start(pos1_sb[:], pos1)
         nc.sync.dma_start(pos2_sb[:], pos2)
-        w1_raw[1, 0] = load_w1(1, 0)
-        w1_raw[1, 1] = load_w1(1, 1)
         nc.sync.dma_start(pos3_sb[:], pos3)
-        load_w2(1)
-        w2_by_row = w2_scales.rearrange("a (q r) c -> r q a c", r=4)
-        for r in range(4):
-            nc.gpsimd.dma_start(out=w2_scale_rows[r:P:32, :, :].bitcast(I32), in_=w2_by_row[r].bitcast(I32))
         nc.vector.tensor_copy(v_picked_scales[:], tab_scale_rows[:].indirect(offs_sb[:]))
-        for a in range(GROUPS):
-            for quadrant in range(4):
-                move_scale_rows(a, quadrant)
+        tab_win[1] = load_table(1)
+        move_scale_rows(0)
 
         con_win = []
         for s in range(GROUPS * PACK):
@@ -121,7 +113,7 @@ def tile_list_ballot_contest_codes_kernel(
             nc.vector.memset(win[:, PAIRS:], 0.0)
             con_win.append(win)
 
-        gain_sq = keep.tile([P, GROUPS, PACK], F32, name="gain_sq")
+        gain_sq = ring.tile([P, GROUPS, PACK], F32, name="gain_sq", tag="w1_rows1", bufs=1)
         sv_gain = keep.tile([P, GROUPS, PACK], F32, name="sv_gain")
         nc.vector.tensor_tensor(gain_sq[:], gain_sb[:], gain_sb[:], ALU.mult)
         nc.vector.tensor_tensor(sv_gain[:], sv_sb[:], gain_sb[:], ALU.mult)
@@ -129,6 +121,8 @@ def tile_list_ballot_contest_codes_kernel(
         for b in range(GROUPS):
             for t in range(PACK):
                 nc.vector.tensor_copy(gain_sq_wide[:, b, t, :], gain_sq[:, b, t : t + 1].to_broadcast([P, PAIR_PIECE]))
+        w1_raw[0, 1] = load_w1(0, 1)
+        move_scale_rows(1)
 
         v_words = [keep.tile([P, S], I32, name="v_words%d" % a, align_bytes=64) for a in range(GROUPS)]
 
@@ -163,8 +157,8 @@ def tile_list_ballot_contest_codes_kernel(
 
         def first_product(b):
             banks = {}
-            for a in range(GROUPS):
-                for t in range(PACK):
+            for t in range(PACK):
+                for a in range(GROUPS):
                     for half in range(S // BANK):
                         if a == 0:
                             banks[t, half] = psum.tile([P, BANK], F32, name="bank", tag="bank")
@@ -174,7 +168,7 @@ def tile_list_ballot_contest_codes_kernel(
                             lhsT=w1_codes[b, a][:, t, :].bitcast(FP8X4),
                             lhsT_scale=w1_scales[b, a][:, t, :],
                             rhs=v_words[a][:, cols].bitcast(FP8X4),
-                            rhs_scale=v_scales[4 * a :, cols],
+                            rhs_scale=v_scales[a][:, cols],
                             start=(a == 0),
                             stop=(a == GROUPS - 1),
                         )
@@ -188,7 +182,7 @@ def tile_list_ballot_contest_codes_kernel(
 
         def pair_products(b, t, tag="first", bufs=2):
             if t == 0:
-                z_rows[b] = ring.tile([P, PACK, PAIRS], F32, name="z_rows", tag="rows", bufs=5)
+                z_rows[b] = ring.tile([P, PACK, PAIRS], F32, name="z_rows", tag="rows", bufs=4)
             first = ring.tile([P, PAIRS], F32, name="first", tag=tag, bufs=bufs, align_bytes=64)
             for m0 in range(0, PAIRS, PAIR_PIECE):
                 window = tanh_rows[b, t][:].indirect(entries(pos1_sb, m0, m0 + PAIR_PIECE))
@@ -221,14 +215,14 @@ def tile_list_ballot_contest_codes_kernel(
             nc.vector.tensor_copy(words[:], w2_raw[b][:].rearrange("p a (q t e) -> p a t q e", t=PACK, e=2))
             w2_dealt[b] = words
 
-        def deal_w2_scales():
+        def deal_w2_scales(w2_scale_rows):
             src = w2_scale_rows[:].rearrange("p a (b q t) -> p (a b) t q", b=GROUPS, t=PACK)
             nc.vector.tensor_copy(w2_dealt_scales[:], src)
 
         def second_product(b):
             banks = {}
-            for a in range(GROUPS):
-                for t in range(PACK):
+            for t in range(PACK):
+                for a in range(GROUPS):
                     if a == 0:
                         banks[t] = psum.tile([P, BANK], F32, name="bank", tag="bank")
                     nc.tensor.matmul_mx(
@@ -247,7 +241,7 @@ def tile_list_ballot_contest_codes_kernel(
 
         def make_one_plus_own(b, slices):
             if b not in one_plus_own:
-                one_plus_own[b] = ring.tile([P, PACK, S], F32, name="one_plus_own", tag="wide", bufs=2)
+                one_plus_own[b] = ring.tile([P, PACK, S], F32, name="one_plus_own", tag="wide", bufs=2, align_bytes=64)
             for t in slices:
                 nc.scalar.activation(
                     one_plus_own[b][:, t, :], tanh_rows[b, t][:], ACT.Identity, bias=1.0, scale=sv_gain[:, b, t : t + 1]
@@ -255,16 +249,25 @@ def tile_list_ballot_contest_codes_kernel(
 
         gather_words(0)
         deal_w2(0, "dealt0")
-        quantise_w1(0, 0, round_w1(0, 0, 0, "woven", 3))
+        quantise_w1(0, 0, round_w1(0, 0, 0, "hold0", 1))
+        w2_scale_rows = ring.tile([P, GROUPS, H], U8, name="w2_scale_rows", tag="hold0", bufs=1, align_bytes=64)
+        nc.vector.memset(w2_scale_rows[:].rearrange("p a c -> p (a c)").bitcast(I32), 0)
+        w2_by_row = w2_scales.rearrange("a (q r) c -> r q a c", r=4)
+        for r in range(4):
+            nc.sync.dma_start(out=w2_scale_rows[r:P:32, :, :].bitcast(I32), in_=w2_by_row[r].bitcast(I32))
         gather_words(1)
-        quantise_w1(0, 1, round_w1(0, 1, VECTOR_SHARE, "woven", 3))
-        deal_w2_scales()
+        quantise_w1(0, 1, round_w1(0, 1, VECTOR_SHARE, "hold2", 1))
+        w1_raw[1, 0] = load_w1(1, 0)
+        w1_raw[1, 1] = load_w1(1, 1)
+        load_w2(1, "hold2")
+        deal_w2_scales(w2_scale_rows)
         first_product(0)
-        dealt_10 = round_w1(1, 0, 0, "codes00", 1)
-        dealt_11 = round_w1(1, 1, 48, "codes01", 1)
-        for t in range(PACK - 1):
+        dealt_10 = round_w1(1, 0, 48, "codes00", 1)
+        dealt_11 = round_w1(1, 1, 0, "codes01", 1)
+        for t in range(PACK - 2):
             pair_products(0, t)
         quantise_w1(1, 0, dealt_10)
+        pair_products(0, PACK - 2, "codes00", 1)
         quantise_w1(1, 1, dealt_11)
         pair_products(0, PACK - 1, "codes01", 1)
         first_product(1)
@@ -294,7 +297,7 @@ def tile_list_ballot_contest_codes_kernel(
 
         def add_own(b, j0, j1, t):
             if t == 0:
-                y_rows[b, j0] = ring.tile([P, PACK, j1 - j0], F32, name="y_rows", tag="rows", bufs=5)
+                y_rows[b, j0] = ring.tile([P, PACK, j1 - j0], F32, name="y_rows", tag="rows", bufs=4)
             nc.vector.scalar_tensor_tensor(
                 out=y_rows[b, j0][:, t, :],
                 in0=tanh_rows[b, t][:, j0:j1],

from contextlib import ExitStack

import concourse.mybir as mybir

K, T, S, H, PAIRS = 1024, 4096, 1024, 1024, 512
FLOPS = 2 * K * H * S + 2 * H * H * PAIRS

F32 = mybir.dt.float32
BF16 = mybir.dt.bfloat16
I32 = mybir.dt.int32
U32 = mybir.dt.uint32
U16 = mybir.dt.uint16
U8 = mybir.dt.uint8
FP8X4 = mybir.dt.float8_e4m3fn_x4
FP4X4 = mybir.dt.float4_e2m1fn_x4
ACT = mybir.ActivationFunctionType
ALU = mybir.AluOpType

P = 128
PACK = 4
GROUP = P * PACK
GROUPS = 2
BANK = 512
LIST_ROWS = 16
PAIR_PIECE = 256
CON_WINDOW = PAIRS + 32
VECTOR_SHARE = 88
OUT_PIECES = (((0, 512), (512, 1024)), ((0, 512), (512, 768), (768, 1024)))


def entries(offsets, first, last):
    return offsets[:, first // LIST_ROWS : last // LIST_ROWS]


def weave(engine_copy, woven, rows):
    engine_copy(
        out=woven.rearrange("p (c t) -> p c t", t=PACK),
        in_=rows.rearrange("p t c -> p c t"),
    )


def tile_list_ballot_contest_codes_kernel(
    tc, tab_words, tab_scales, offs, pos1, pos2, pos3, w1, gain, w2_words, w2_scales, sv, out_0, out_1, out_2
):
    nc = tc.nc
    with ExitStack() as ctx:
        keep = ctx.enter_context(tc.tile_pool(name="keep", bufs=1))
        ring = ctx.enter_context(tc.tile_pool(name="ring", bufs=1))
        psum = ctx.enter_context(tc.psum_pool(name="psum", bufs=8))

        offs_sb = keep.tile([P, S // LIST_ROWS], U16, name="offs_sb")
        pos1_sb = keep.tile([P, PAIRS // LIST_ROWS], U16, name="pos1_sb")
        pos2_sb = keep.tile([P, PAIRS // LIST_ROWS], U16, name="pos2_sb")
        pos3_sb = keep.tile([P, S // LIST_ROWS], U16, name="pos3_sb")
        gain_sb = keep.tile([P, GROUPS, PACK], F32, name="gain_sb")
        sv_sb = keep.tile([P, GROUPS, PACK], F32, name="sv_sb")
        tab_scale_rows = ring.tile([P, T], U8, name="tab_scale_rows", tag="wide", bufs=2, align_bytes=64)
        w2_raw = {}

        def load_w2(b, tag):
            w2_raw[b] = ring.tile([P, GROUPS, 2 * GROUP], U8, name="w2_raw", tag=tag, bufs=1, align_bytes=64)
            block = w2_words[:, :, 2 * b * GROUP : 2 * (b + 1) * GROUP].rearrange("a p c -> p a c")
            nc.sync.dma_start(out=w2_raw[b][:].bitcast(I32), in_=block.bitcast(I32))

        def load_table(a):
            words = ring.tile([P, T], I32, name="tab_win", tag="wide", bufs=2, align_bytes=64)
            nc.sync.dma_start(out=words[:], in_=tab_words[a].rearrange("p t i -> p (t i)").bitcast(I32))
            return words

        def load_w1(b, a):
            raw = ring.tile([P, PACK, GROUP], F32, name="w1_raw", tag="w1_rows%d" % a, bufs=1)
            block = w1[a * GROUP : (a + 1) * GROUP, b * GROUP : (b + 1) * GROUP]
            nc.sync.dma_start(out=raw[:], in_=block.rearrange("(p j) c -> p j c", j=PACK))
            return raw

        nc.vector.memset(tab_scale_rows[32:64, :].bitcast(I32), 0)
        nc.vector.memset(tab_scale_rows[64:, :].bitcast(I32), 0)
        v_picked_scales = keep.tile([P, S], U8, name="v_picked_scales", align_bytes=64)
        v_scales = [keep.tile([P, S], U8, name="v_scales%d" % a, align_bytes=64) for a in range(GROUPS)]
        for a in range(GROUPS):
            nc.vector.memset(v_scales[a][:].bitcast(I32), 0)

        tab_win = {}
        w1_raw = {}

        def move_scale_rows(a):
            for quadrant in range(4):
                src = 16 * a + 4 * quadrant
                dst = 32 * quadrant
                nc.sync.dma_start(
                    out=v_scales[a][dst : dst + 4, :].bitcast(I32), in_=v_picked_scales[src : src + 4, :].bitcast(I32)
                )

        nc.sync.dma_start(
            out=tab_scale_rows[:32, :].bitcast(I32), in_=tab_scales.rearrange("a q t -> (a q) t").bitcast(I32)
        )
        nc.sync.dma_start(offs_sb[:], offs)
        tab_win[0] = load_table(0)
        load_w2(0, "w2_raw0")
        w1_raw[0, 0] = load_w1(0, 0)
        nc.sync.dma_start(out=gain_sb[:], in_=gain.rearrange("(b p t) -> p b t", b=GROUPS, t=PACK))
        nc.sync.dma_start(out=sv_sb[:], in_=sv.rearrange("(b p t) -> p b t", b=GROUPS, t=PACK))
        nc.sync.dma_start(pos1_sb[:], pos1)
        nc.sync.dma_start(pos2_sb[:], pos2)
        nc.sync.dma_start(pos3_sb[:], pos3)
        nc.vector.tensor_copy(v_picked_scales[:], tab_scale_rows[:].indirect(offs_sb[:]))
        tab_win[1] = load_table(1)
        move_scale_rows(0)

        con_win = []
        for s in range(GROUPS * PACK):
            win = keep.tile([P, CON_WINDOW], F32, name="con_win%d" % s)
            nc.vector.memset(win[:, PAIRS:], 0.0)
            con_win.append(win)

        gain_sq = ring.tile([P, GROUPS, PACK], F32, name="gain_sq", tag="w1_rows1", bufs=1)
        sv_gain = keep.tile([P, GROUPS, PACK], F32, name="sv_gain")
        nc.vector.tensor_tensor(gain_sq[:], gain_sb[:], gain_sb[:], ALU.mult)
        nc.vector.tensor_tensor(sv_gain[:], sv_sb[:], gain_sb[:], ALU.mult)
        gain_sq_wide = keep.tile([P, GROUPS, PACK, PAIR_PIECE], F32, name="gain_sq_wide")
        for b in range(GROUPS):
            for t in range(PACK):
                nc.vector.tensor_copy(gain_sq_wide[:, b, t, :], gain_sq[:, b, t : t + 1].to_broadcast([P, PAIR_PIECE]))
        w1_raw[0, 1] = load_w1(0, 1)
        move_scale_rows(1)

        v_words = [keep.tile([P, S], I32, name="v_words%d" % a, align_bytes=64) for a in range(GROUPS)]

        def gather_words(a):
            nc.vector.tensor_copy(v_words[a][:].bitcast(U32), tab_win[a][:].bitcast(U32).indirect(offs_sb[:]))

        w1_codes = {}
        w1_scales = {}

        def round_w1(b, a, vector_share, tag, bufs):
            dealt = ring.tile([P, PACK, P, PACK], BF16, name="w1_dealt", tag=tag, bufs=bufs, align_bytes=64)
            dst = dealt[:].rearrange("p t q j -> p q t j")
            src = w1_raw[b, a][:].rearrange("p j (q t) -> p q t j", t=PACK)
            if vector_share:
                nc.vector.tensor_copy(dst[:, :vector_share], src[:, :vector_share])
            nc.scalar.copy(dst[:, vector_share:], src[:, vector_share:])
            return dealt

        def quantise_w1(b, a, dealt):
            codes = ring.tile([P, PACK, P], I32, name="w1_codes", tag="codes%d%d" % (b, a), bufs=1, align_bytes=64)
            scales = keep.tile([P, PACK, P], U8, name="w1_scales%d%d" % (b, a), align_bytes=64)
            for t in range(PACK):
                nc.vector.quantize_mx(
                    out=codes[:, t, :].bitcast(FP8X4),
                    scales=scales[:, t, :],
                    in_=dealt[:, t].rearrange("p q j -> p (q j)"),
                )
            w1_codes[b, a] = codes
            w1_scales[b, a] = scales

        tanh_rows = {}

        def first_product(b):
            banks = {}
            for t in range(PACK):
                for a in range(GROUPS):
                    for half in range(S // BANK):
                        if a == 0:
                            banks[t, half] = psum.tile([P, BANK], F32, name="bank", tag="bank")
                        cols = slice(half * BANK, (half + 1) * BANK)
                        nc.tensor.matmul_mx(
                            out=banks[t, half][:],
                            lhsT=w1_codes[b, a][:, t, :].bitcast(FP8X4),
                            lhsT_scale=w1_scales[b, a][:, t, :],
                            rhs=v_words[a][:, cols].bitcast(FP8X4),
                            rhs_scale=v_scales[a][:, cols],
                            start=(a == 0),
                            stop=(a == GROUPS - 1),
                        )
            for t in range(PACK):
                rows = keep.tile([P, S], F32, name="tanh_rows%d%d" % (b, t))
                for half in range(S // BANK):
                    nc.scalar.activation(rows[:, half * BANK : (half + 1) * BANK], banks[t, half][:], ACT.Tanh)
                tanh_rows[b, t] = rows

        z_rows = {}

        def pair_products(b, t, tag="first", bufs=2):
            if t == 0:
                z_rows[b] = ring.tile([P, PACK, PAIRS], F32, name="z_rows", tag="rows", bufs=4)
            first = ring.tile([P, PAIRS], F32, name="first", tag=tag, bufs=bufs, align_bytes=64)
            for m0 in range(0, PAIRS, PAIR_PIECE):
                window = tanh_rows[b, t][:].indirect(entries(pos1_sb, m0, m0 + PAIR_PIECE))
                nc.vector.tensor_tensor(first[:, m0 : m0 + PAIR_PIECE], window, gain_sq_wide[:, b, t, :], ALU.mult)
            for m0 in range(0, PAIRS, PAIR_PIECE):
                window = tanh_rows[b, t][:].indirect(entries(pos2_sb, m0, m0 + PAIR_PIECE))
                nc.vector.tensor_tensor(
                    z_rows[b][:, t, m0 : m0 + PAIR_PIECE], window, first[:, m0 : m0 + PAIR_PIECE], ALU.mult
                )

        z_codes = [keep.tile([P, PAIRS], I32, name="z_codes%d" % b, align_bytes=64) for b in range(GROUPS)]
        z_scales = [keep.tile([P, PAIRS], U8, name="z_scales%d" % b, align_bytes=64) for b in range(GROUPS)]

        def quantise_z(b, copies, tag, bufs):
            woven = ring.tile([P, PAIRS * PACK], BF16, name="z_woven", tag=tag, bufs=bufs, align_bytes=64)
            for m0, engine_copy in zip(range(0, PAIRS, PAIR_PIECE), copies):
                weave(engine_copy, woven[:, m0 * PACK : (m0 + PAIR_PIECE) * PACK], z_rows[b][:, :, m0 : m0 + PAIR_PIECE])
            for m0 in range(0, PAIRS, PAIR_PIECE):
                nc.vector.quantize_mx(
                    out=z_codes[b][:, m0 : m0 + PAIR_PIECE].bitcast(FP8X4),
                    scales=z_scales[b][:, m0 : m0 + PAIR_PIECE],
                    in_=woven[:, m0 * PACK : (m0 + PAIR_PIECE) * PACK],
                )

        w2_dealt = {}
        w2_dealt_scales = keep.tile([P, GROUPS * GROUPS, PACK, P], U8, name="w2_dealt_scales", align_bytes=64)

        def deal_w2(b, tag):
            words = ring.tile([P, GROUPS, PACK, P, 2], U8, name="w2_dealt", tag=tag, bufs=1, align_bytes=64)
            nc.vector.tensor_copy(words[:], w2_raw[b][:].rearrange("p a (q t e) -> p a t q e", t=PACK, e=2))
            w2_dealt[b] = words

        def deal_w2_scales(w2_scale_rows):
            src = w2_scale_rows[:].rearrange("p a (b q t) -> p (a b) t q", b=GROUPS, t=PACK)
            nc.vector.tensor_copy(w2_dealt_scales[:], src)

        def second_product(b):
            banks = {}
            for t in range(PACK):
                for a in range(GROUPS):
                    if a == 0:
                        banks[t] = psum.tile([P, BANK], F32, name="bank", tag="bank")
                    nc.tensor.matmul_mx(
                        out=banks[t][:],
                        lhsT=w2_dealt[b][:, a, t].rearrange("p q e -> p (q e)").bitcast(FP4X4),
                        lhsT_scale=w2_dealt_scales[:, a * GROUPS + b, t, :],
                        rhs=z_codes[a][:].bitcast(FP8X4),
                        rhs_scale=z_scales[a][:],
                        start=(a == 0),
                        stop=(a == GROUPS - 1),
                    )
            for t in range(PACK):
                nc.scalar.copy(con_win[b * PACK + t][:, :PAIRS], banks[t][:])

        one_plus_own = {}

        def make_one_plus_own(b, slices):
            if b not in one_plus_own:
                one_plus_own[b] = ring.tile([P, PACK, S], F32, name="one_plus_own", tag="wide", bufs=2, align_bytes=64)
            for t in slices:
                nc.scalar.activation(
                    one_plus_own[b][:, t, :], tanh_rows[b, t][:], ACT.Identity, bias=1.0, scale=sv_gain[:, b, t : t + 1]
                )

        gather_words(0)
        deal_w2(0, "dealt0")
        quantise_w1(0, 0, round_w1(0, 0, 0, "hold0", 1))
        w2_scale_rows = ring.tile([P, GROUPS, H], U8, name="w2_scale_rows", tag="hold0", bufs=1, align_bytes=64)
        nc.vector.memset(w2_scale_rows[:].rearrange("p a c -> p (a c)").bitcast(I32), 0)
        w2_by_row = w2_scales.rearrange("a (q r) c -> r q a c", r=4)
        for r in range(4):
            nc.sync.dma_start(out=w2_scale_rows[r:P:32, :, :].bitcast(I32), in_=w2_by_row[r].bitcast(I32))
        gather_words(1)
        quantise_w1(0, 1, round_w1(0, 1, VECTOR_SHARE, "hold2", 1))
        w1_raw[1, 0] = load_w1(1, 0)
        w1_raw[1, 1] = load_w1(1, 1)
        load_w2(1, "hold2")
        deal_w2_scales(w2_scale_rows)
        first_product(0)
        dealt_10 = round_w1(1, 0, 48, "codes00", 1)
        dealt_11 = round_w1(1, 1, 0, "codes01", 1)
        for t in range(PACK - 2):
            pair_products(0, t)
        quantise_w1(1, 0, dealt_10)
        pair_products(0, PACK - 2, "codes00", 1)
        quantise_w1(1, 1, dealt_11)
        pair_products(0, PACK - 1, "codes01", 1)
        first_product(1)
        for t in range(PACK - 1):
            pair_products(1, t)
        quantise_z(0, (nc.scalar.copy, nc.scalar.copy), "hold0", 1)
        pair_products(1, PACK - 1, "hold0", 1)
        make_one_plus_own(0, range(PACK - 1))
        quantise_z(1, (nc.scalar.copy, nc.vector.tensor_copy), "hold1", 1)
        deal_w2(1, "hold1")
        second_product(0)
        make_one_plus_own(0, range(PACK - 1, PACK))
        second_product(1)
        make_one_plus_own(1, range(PACK))

        y_scales = [keep.tile([P, S], U8, name="y_scales%d" % b, align_bytes=64) for b in range(GROUPS)]
        steps = [(b, j0, j1, t) for b in range(GROUPS) for (j0, j1) in OUT_PIECES[b] for t in range(PACK)]
        y_rows = {}
        raised = {}
        y_woven = {}

        def raise_code(b, j0, j1, t):
            prod = ring.tile([P, j1 - j0], F32, name="raised", tag="raised", bufs=3)
            window = con_win[b * PACK + t][:].indirect(entries(pos3_sb, j0, j1))
            nc.vector.tensor_tensor(prod[:], window, one_plus_own[b][:, t, j0:j1], ALU.mult)
            raised[b, j0, t] = prod

        def add_own(b, j0, j1, t):
            if t == 0:
                y_rows[b, j0] = ring.tile([P, PACK, j1 - j0], F32, name="y_rows", tag="rows", bufs=4)
            nc.vector.scalar_tensor_tensor(
                out=y_rows[b, j0][:, t, :],
                in0=tanh_rows[b, t][:, j0:j1],
                scalar=sv_gain[:, b, t : t + 1],
                in1=raised[b, j0, t][:],
                op0=ALU.mult,
                op1=ALU.add,
            )
            out_rows = out_0[b * GROUP : (b + 1) * GROUP, j0:j1].rearrange("(p t) j -> t p j", t=PACK)
            nc.sync.dma_start(out=out_rows[t], in_=y_rows[b, j0][:, t, :])

        def round_y(b, j0, j1, engine_copy):
            woven = ring.tile([P, (j1 - j0) * PACK], BF16, name="y_woven", tag="woven", bufs=3, align_bytes=64)
            weave(engine_copy, woven[:], y_rows[b, j0][:])
            y_woven[b, j0] = woven

        def quantise_y(b, j0, j1):
            codes = ring.tile([P, j1 - j0], I32, name="y_codes", tag="y_codes", bufs=3, align_bytes=64)
            nc.vector.quantize_mx(out=codes[:].bitcast(FP8X4), scales=y_scales[b][:, j0:j1], in_=y_woven[b, j0][:])
            words = out_1[b, :, j0:j1, :].rearrange("p m t -> p (m t)").bitcast(I32)
            nc.sync.dma_start(out=words, in_=codes[:])
            if j1 == S:
                by_row = out_2[b].rearrange("(q r) m -> r q m", r=4)
                for r in range(4):
                    queue = nc.scalar if r % 2 else nc.sync
                    queue.dma_start(out=by_row[r].bitcast(I32), in_=y_scales[b][r:P:32, :].bitcast(I32))

        raise_code(*steps[0])
        waiting = None
        for i, (b, j0, j1, t) in enumerate(steps):
            if i + 1 < len(steps):
                raise_code(*steps[i + 1])
            add_own(b, j0, j1, t)
            if t == PACK - 1:
                if waiting is not None:
                    quantise_y(*waiting)
                last = i + 1 == len(steps)
                round_y(b, j0, j1, nc.vector.tensor_copy if last else nc.scalar.copy)
                waiting = (b, j0, j1)
        quantise_y(*waiting)
